import numpy as np
import ml_dtypes


def mxq(x, axis, fmt="e4m3"):
    dtype, down = {"e4m3": (ml_dtypes.float8_e4m3fn, 7), "e5m2": (ml_dtypes.float8_e5m2, 14)}[fmt]
    v = np.moveaxis(np.asarray(x, np.float32).astype(ml_dtypes.bfloat16).astype(np.float64), axis, -1)
    blocks = v.reshape(v.shape[:-1] + (-1, 32))
    amax = np.abs(blocks).max(-1, keepdims=True)
    byte = np.maximum(np.where(amax > 0, np.frexp(amax)[1] - 1 + 127, 0) - down, 1)
    scale = np.exp2(byte - 127.0)
    codes = (blocks / scale).astype(np.float32).astype(dtype).astype(np.float64)
    return np.moveaxis((codes * scale).reshape(v.shape), -1, axis)


WIDE = False


def mx_kscale(k):
    if not WIDE:
        return np.ones(k)
    levels = np.array([10, -10, 5, -5, 0])
    if k % 512:
        return np.exp2(np.random.permutation(np.resize(levels, k // 32))).repeat(32)
    a = np.empty((k // 512, 16))
    for p in range(k // 512):
        a[p, :8] = np.random.permutation(np.resize(levels, 8))
        for g in range(8):
            far = levels[np.abs(levels - a[p, g]) >= 10]
            a[p, g + 8] = far[np.random.randint(len(far))]
    return np.exp2(a.ravel()).repeat(32)


def f64(x):
    return np.asarray(x).astype(np.float64)


def striped(idx):
    return np.tile(idx.reshape(-1, 16).T, (8, 1)).astype(np.uint16)


def unstriped(offs):
    return offs[:16].T.reshape(-1).astype(np.int64)


K, T, E, C, N = 512, 2048, 8, 128, 128


def by_expert(wq, xq):
    return np.concatenate([wq[e].T @ xq[:, e * C:(e + 1) * C] for e in range(E)], axis=1)


def setup_inputs():
    n = np.random.standard_normal
    s = mx_kscale(K)[:, None]
    return {
        "xT": (n((K, T)) * s).astype(np.float32),
        "w": (n((E, K, N)) / np.sqrt(K) / s[None]).astype(np.float32),
        "gate": np.tile(np.random.uniform(0.2, 1.0, E * C), (N, 1)).astype(np.float32),
        "offs": striped(np.random.permutation(T)[:E * C]),
    }


def reference(xT, w, gate, offs):
    idx = unstriped(offs)
    xq = mxq(f64(xT)[:, idx], 0, "e4m3")
    y = by_expert(mxq(f64(w), 1, "e4m3"), xq)
    out = np.zeros((N, T))
    out[:, idx] = f64(gate) * y
    return out

@@ -1,0 +1,108 @@
+from contextlib import ExitStack
+
+import concourse.mybir as mybir
+
+K, T, E, C, N = 512, 2048, 8, 128, 128
+SLOTS = E * C
+FLOPS = 2 * K * N * SLOTS
+
+F32 = mybir.dt.float32
+BF16 = mybir.dt.bfloat16
+U32 = mybir.dt.uint32
+U16 = mybir.dt.uint16
+U8 = mybir.dt.uint8
+FP8X4 = mybir.dt.float8_e4m3fn_x4
+MULT = mybir.AluOpType.mult
+
+P = 128
+PACK = 4
+CHUNK = 256
+N_CHUNKS = SLOTS // CHUNK
+E_CHUNK = CHUNK // C
+OFF_COLS = CHUNK // 16
+
+W_ON_VECTOR = (0, 1)
+
+
+def tile_routed_moe_kernel(tc, xT, w, gate, offs, out):
+    nc = tc.nc
+    with ExitStack() as ctx:
+        held = ctx.enter_context(tc.tile_pool(name="held", bufs=1))
+        psum = ctx.enter_context(tc.psum_pool(name="psum", bufs=1))
+
+        offsets = held.tile([P, SLOTS // 16], U16, name="offsets")
+        nc.sync.dma_start(offsets[:], offs)
+
+        x_rows = xT.rearrange("(p t) n -> p t n", t=PACK)
+        x_planes = []
+        for t in range(PACK):
+            plane = held.tile([P, T], F32, name="x_plane%d" % t)
+            nc.sync.dma_start(plane[:], x_rows[:, t, :])
+            x_planes.append(plane)
+
+        w_rows = w.rearrange("e (p j) n -> p e j n", j=PACK)
+        w_raw = []
+        gate_sb = []
+        for c in range(N_CHUNKS):
+            raw = held.tile([P, E_CHUNK, PACK, N], F32, name="w_raw%d" % c)
+            nc.sync.dma_start(raw[:], w_rows[:, c * E_CHUNK : (c + 1) * E_CHUNK, :, :])
+            w_raw.append(raw)
+            g = held.tile([P, CHUNK], F32, name="gate%d" % c)
+            nc.sync.dma_start(g[:], gate[:, c * CHUNK : (c + 1) * CHUNK])
+            gate_sb.append(g)
+
+        window = held.tile([P, T], F32, name="window")
+        nc.vector.memset(window[:], 0.0)
+
+        def offs_of(c):
+            return offsets[:, c * OFF_COLS : (c + 1) * OFF_COLS]
+
+        gathered = [held.tile([P, PACK, CHUNK], F32, name="gathered%d" % c) for c in range(N_CHUNKS)]
+        for t in range(PACK):
+            for c in range(N_CHUNKS):
+                nc.vector.tensor_copy(gathered[c][:, t, :], x_planes[t][:].indirect(offs_of(c)))
+
+        for c in range(N_CHUNKS):
+            x_grouped = held.tile([P, CHUNK, PACK], BF16, name="x_grouped%d" % c, align_bytes=64)
+            nc.scalar.copy(out=x_grouped[:], in_=gathered[c][:].rearrange("p t n -> p n t"))
+
+            w_grouped = held.tile([P, CHUNK, PACK], BF16, name="w_grouped%d" % c, align_bytes=64)
+            w_out = w_grouped[:].rearrange("p (e n) j -> p e n j", e=E_CHUNK)
+            w_in = w_raw[c][:].rearrange("p e j n -> p e n j")
+            if c in W_ON_VECTOR:
+                nc.vector.tensor_copy(out=w_out, in_=w_in)
+            else:
+                nc.scalar.copy(out=w_out, in_=w_in)
+
+            x_codes = held.tile([P, CHUNK], U32, name="x_codes%d" % c, align_bytes=64)
+            x_scales = held.tile([P, CHUNK], U8, name="x_scales%d" % c, align_bytes=64)
+            nc.vector.quantize_mx(
+                out=x_codes[:].bitcast(FP8X4),
+                scales=x_scales[:],
+                in_=x_grouped[:].rearrange("p n t -> p (n t)"),
+            )
+            w_codes = held.tile([P, CHUNK], U32, name="w_codes%d" % c, align_bytes=64)
+            w_scales = held.tile([P, CHUNK], U8, name="w_scales%d" % c, align_bytes=64)
+            nc.vector.quantize_mx(
+                out=w_codes[:].bitcast(FP8X4),
+                scales=w_scales[:],
+                in_=w_grouped[:].rearrange("p n j -> p (n j)"),
+            )
+
+            sums = psum.tile([P, CHUNK], F32, name="sums%d" % c)
+            for i in range(E_CHUNK):
+                cols = slice(i * C, (i + 1) * C)
+                nc.tensor.matmul_mx(
+                    out=sums[:, cols],
+                    lhsT=w_codes[:, cols].bitcast(FP8X4),
+                    lhsT_scale=w_scales[:, cols],
+                    rhs=x_codes[:, cols].bitcast(FP8X4),
+                    rhs_scale=x_scales[:, cols],
+                    start=True,
+                    stop=True,
+                )
+            sums_sb = held.tile([P, CHUNK], F32, name="sums_sb%d" % c)
+            nc.scalar.copy(out=sums_sb[:], in_=sums[:])
+            nc.vector.tensor_tensor(window[:].indirect(offs_of(c)), sums_sb[:], gate_sb[c][:], MULT)
+
+        nc.sync.dma_start(out, window[:])

@@ -19,9 +19,9 @@ PACK = 4
 CHUNK = 256
 N_CHUNKS = SLOTS // CHUNK
 E_CHUNK = CHUNK // C
-OFF_COLS = CHUNK // 16
+EARLY = 512
 
-W_ON_VECTOR = (0, 1)
+W_ON_VECTOR = (0,)
 
 
 def tile_routed_moe_kernel(tc, xT, w, gate, offs, out):
@@ -54,17 +54,30 @@ def tile_routed_moe_kernel(tc, xT, w, gate, offs, out):
         window = held.tile([P, T], F32, name="window")
         nc.vector.memset(window[:], 0.0)
 
-        def offs_of(c):
-            return offsets[:, c * OFF_COLS : (c + 1) * OFF_COLS]
+        def offs_of(first_slot, n_slots):
+            return offsets[:, first_slot // 16 : (first_slot + n_slots) // 16]
 
-        gathered = [held.tile([P, PACK, CHUNK], F32, name="gathered%d" % c) for c in range(N_CHUNKS)]
-        for t in range(PACK):
+        early = [held.tile([P, 2, EARLY], F32, name="early%d" % h) for h in range(SLOTS // EARLY)]
+        for t in range(2):
+            for h in range(SLOTS // EARLY):
+                nc.vector.tensor_copy(early[h][:, t, :], x_planes[t][:].indirect(offs_of(h * EARLY, EARLY)))
+
+        x_grouped = [
+            held.tile([P, CHUNK, PACK], BF16, name="x_grouped%d" % c, align_bytes=64) for c in range(N_CHUNKS)
+        ]
+        for c in range(N_CHUNKS):
+            nc.scalar.copy(
+                out=x_grouped[c][:, :, 0:2],
+                in_=early[c * CHUNK // EARLY][:, :, c * CHUNK % EARLY : c * CHUNK % EARLY + CHUNK].rearrange("p t n -> p n t"),
+            )
+
+        late = [held.tile([P, 2, CHUNK], F32, name="late%d" % c) for c in range(N_CHUNKS)]
+        for t in range(2):
             for c in range(N_CHUNKS):
-                nc.vector.tensor_copy(gathered[c][:, t, :], x_planes[t][:].indirect(offs_of(c)))
+                nc.vector.tensor_copy(late[c][:, t, :], x_planes[2 + t][:].indirect(offs_of(c * CHUNK, CHUNK)))
 
         for c in range(N_CHUNKS):
-            x_grouped = held.tile([P, CHUNK, PACK], BF16, name="x_grouped%d" % c, align_bytes=64)
-            nc.scalar.copy(out=x_grouped[:], in_=gathered[c][:].rearrange("p t n -> p n t"))
+            nc.scalar.copy(out=x_grouped[c][:, :, 2:4], in_=late[c][:].rearrange("p t n -> p n t"))
 
             w_grouped = held.tile([P, CHUNK, PACK], BF16, name="w_grouped%d" % c, align_bytes=64)
             w_out = w_grouped[:].rearrange("p (e n) j -> p e n j", e=E_CHUNK)
@@ -79,7 +92,7 @@ def tile_routed_moe_kernel(tc, xT, w, gate, offs, out):
             nc.vector.quantize_mx(
                 out=x_codes[:].bitcast(FP8X4),
                 scales=x_scales[:],
-                in_=x_grouped[:].rearrange("p n t -> p (n t)"),
+                in_=x_grouped[c][:].rearrange("p n t -> p (n t)"),
             )
             w_codes = held.tile([P, CHUNK], U32, name="w_codes%d" % c, align_bytes=64)
             w_scales = held.tile([P, CHUNK], U8, name="w_scales%d" % c, align_bytes=64)
@@ -103,6 +116,6 @@ def tile_routed_moe_kernel(tc, xT, w, gate, offs, out):
                 )
             sums_sb = held.tile([P, CHUNK], F32, name="sums_sb%d" % c)
             nc.scalar.copy(out=sums_sb[:], in_=sums[:])
-            nc.vector.tensor_tensor(window[:].indirect(offs_of(c)), sums_sb[:], gate_sb[c][:], MULT)
+            nc.vector.tensor_tensor(window[:].indirect(offs_of(c * CHUNK, CHUNK)), sums_sb[:], gate_sb[c][:], MULT)
 
         nc.sync.dma_start(out, window[:])

@@ -21,7 +21,9 @@ N_CHUNKS = SLOTS // CHUNK
 E_CHUNK = CHUNK // C
 EARLY = 512
 
+LOADS = [["x",0],["x",1],["x",2],["x",3],["w",0],["g",0],["w",1],["g",1],["w",2],["g",2],["w",3],["g",3]]
 W_ON_VECTOR = (0,)
+W_FIRST = ()
 
 
 def tile_routed_moe_kernel(tc, xT, w, gate, offs, out):
@@ -34,28 +36,52 @@ def tile_routed_moe_kernel(tc, xT, w, gate, offs, out):
         nc.sync.dma_start(offsets[:], offs)
 
         x_rows = xT.rearrange("(p t) n -> p t n", t=PACK)
-        x_planes = []
-        for t in range(PACK):
-            plane = held.tile([P, T], F32, name="x_plane%d" % t)
-            nc.sync.dma_start(plane[:], x_rows[:, t, :])
-            x_planes.append(plane)
-
         w_rows = w.rearrange("e (p j) n -> p e j n", j=PACK)
-        w_raw = []
-        gate_sb = []
-        for c in range(N_CHUNKS):
-            raw = held.tile([P, E_CHUNK, PACK, N], F32, name="w_raw%d" % c)
-            nc.sync.dma_start(raw[:], w_rows[:, c * E_CHUNK : (c + 1) * E_CHUNK, :, :])
-            w_raw.append(raw)
-            g = held.tile([P, CHUNK], F32, name="gate%d" % c)
-            nc.sync.dma_start(g[:], gate[:, c * CHUNK : (c + 1) * CHUNK])
-            gate_sb.append(g)
+        x_planes = {}
+        w_raw = {}
+        gate_sb = {}
+        for kind, i in LOADS:
+            if kind == "x":
+                x_planes[i] = held.tile([P, T], F32, name="x_plane%d" % i)
+                nc.sync.dma_start(x_planes[i][:], x_rows[:, i, :])
+            elif kind == "w":
+                w_raw[i] = held.tile([P, E_CHUNK, PACK, N], F32, name="w_raw%d" % i)
+                nc.sync.dma_start(w_raw[i][:], w_rows[:, i * E_CHUNK : (i + 1) * E_CHUNK, :, :])
+            else:
+                gate_sb[i] = held.tile([P, CHUNK], F32, name="gate%d" % i)
+                nc.sync.dma_start(gate_sb[i][:], gate[:, i * CHUNK : (i + 1) * CHUNK])
 
         window = held.tile([P, T], F32, name="window")
         nc.vector.memset(window[:], 0.0)
 
         def offs_of(first_slot, n_slots):
             return offsets[:, first_slot // 16 : (first_slot + n_slots) // 16]
+
+        w_grouped = {}
+
+        def interleave_w(c):
+            w_grouped[c] = held.tile([P, CHUNK, PACK], BF16, name="w_grouped%d" % c, align_bytes=64)
+            w_out = w_grouped[c][:].rearrange("p (e b i) j -> p e b j i", e=E_CHUNK, i=4)
+            w_in = w_raw[c][:].rearrange("p e j (b i) -> p e b j i", i=4)
+            if c in W_ON_VECTOR:
+                nc.vector.tensor_copy(out=w_out, in_=w_in)
+            else:
+                nc.scalar.copy(out=w_out, in_=w_in)
+
+        w_codes = {}
+        w_scales = {}
+
+        def quantize_w(c):
+            w_codes[c] = held.tile([P, CHUNK], U32, name="w_codes%d" % c, align_bytes=64)
+            w_scales[c] = held.tile([P, CHUNK], U8, name="w_scales%d" % c, align_bytes=64)
+            nc.vector.quantize_mx(
+                out=w_codes[c][:].bitcast(FP8X4),
+                scales=w_scales[c][:],
+                in_=w_grouped[c][:].rearrange("p n j -> p (n j)"),
+            )
+
+        for c in W_FIRST:
+            interleave_w(c)
 
         early = [held.tile([P, 2, EARLY], F32, name="early%d" % h) for h in range(SLOTS // EARLY)]
         for t in range(2):
@@ -66,26 +92,23 @@ def tile_routed_moe_kernel(tc, xT, w, gate, offs, out):
             held.tile([P, CHUNK, PACK], BF16, name="x_grouped%d" % c, align_bytes=64) for c in range(N_CHUNKS)
         ]
         for c in range(N_CHUNKS):
+            first = c * CHUNK % EARLY
             nc.scalar.copy(
                 out=x_grouped[c][:, :, 0:2],
-                in_=early[c * CHUNK // EARLY][:, :, c * CHUNK % EARLY : c * CHUNK % EARLY + CHUNK].rearrange("p t n -> p n t"),
+                in_=early[c * CHUNK // EARLY][:, :, first : first + CHUNK].rearrange("p t n -> p n t"),
             )
 
         late = [held.tile([P, 2, CHUNK], F32, name="late%d" % c) for c in range(N_CHUNKS)]
-        for t in range(2):
-            for c in range(N_CHUNKS):
-                nc.vector.tensor_copy(late[c][:, t, :], x_planes[2 + t][:].indirect(offs_of(c * CHUNK, CHUNK)))
+        for c in range(N_CHUNKS):
+            nc.vector.tensor_copy(late[c][:, 0, :], x_planes[2][:].indirect(offs_of(c * CHUNK, CHUNK)))
+        for c in W_FIRST:
+            quantize_w(c)
 
         for c in range(N_CHUNKS):
+            nc.vector.tensor_copy(late[c][:, 1, :], x_planes[3][:].indirect(offs_of(c * CHUNK, CHUNK)))
             nc.scalar.copy(out=x_grouped[c][:, :, 2:4], in_=late[c][:].rearrange("p t n -> p n t"))
-
-            w_grouped = held.tile([P, CHUNK, PACK], BF16, name="w_grouped%d" % c, align_bytes=64)
-            w_out = w_grouped[:].rearrange("p (e n) j -> p e n j", e=E_CHUNK)
-            w_in = w_raw[c][:].rearrange("p e j n -> p e n j")
-            if c in W_ON_VECTOR:
-                nc.vector.tensor_copy(out=w_out, in_=w_in)
-            else:
-                nc.scalar.copy(out=w_out, in_=w_in)
+            if c not in W_FIRST:
+                interleave_w(c)
 
             x_codes = held.tile([P, CHUNK], U32, name="x_codes%d" % c, align_bytes=64)
             x_scales = held.tile([P, CHUNK], U8, name="x_scales%d" % c, align_bytes=64)
@@ -94,21 +117,16 @@ def tile_routed_moe_kernel(tc, xT, w, gate, offs, out):
                 scales=x_scales[:],
                 in_=x_grouped[c][:].rearrange("p n t -> p (n t)"),
             )
-            w_codes = held.tile([P, CHUNK], U32, name="w_codes%d" % c, align_bytes=64)
-            w_scales = held.tile([P, CHUNK], U8, name="w_scales%d" % c, align_bytes=64)
-            nc.vector.quantize_mx(
-                out=w_codes[:].bitcast(FP8X4),
-                scales=w_scales[:],
-                in_=w_grouped[:].rearrange("p n j -> p (n j)"),
-            )
+            if c not in W_FIRST:
+                quantize_w(c)
 
             sums = psum.tile([P, CHUNK], F32, name="sums%d" % c)
             for i in range(E_CHUNK):
                 cols = slice(i * C, (i + 1) * C)
                 nc.tensor.matmul_mx(
                     out=sums[:, cols],
-                    lhsT=w_codes[:, cols].bitcast(FP8X4),
-                    lhsT_scale=w_scales[:, cols],
+                    lhsT=w_codes[c][:, cols].bitcast(FP8X4),
+                    lhsT_scale=w_scales[c][:, cols],
                     rhs=x_codes[:, cols].bitcast(FP8X4),
                     rhs_scale=x_scales[:, cols],
                     start=True,

@@ -21,9 +21,9 @@ N_CHUNKS = SLOTS // CHUNK
 E_CHUNK = CHUNK // C
 EARLY = 512
 
-LOADS = [["x",0],["x",1],["x",2],["x",3],["w",0],["g",0],["w",1],["g",1],["w",2],["g",2],["w",3],["g",3]]
-W_ON_VECTOR = (0,)
-W_FIRST = ()
+LOADS = [["x",0],["x",1],["x",2],["w",0],["x",3],["w",1],["w",2],["g",0],["w",3],["g",1],["g",2],["g",3]]
+W_ON_VECTOR = ()
+W_FIRST = (0,)
 
 
 def tile_routed_moe_kernel(tc, xT, w, gate, offs, out):

@@ -16,14 +16,14 @@ MULT = mybir.AluOpType.mult
 
 P = 128
 PACK = 4
+EARLY = 512
 CHUNK = 256
 N_CHUNKS = SLOTS // CHUNK
 E_CHUNK = CHUNK // C
-EARLY = 512
 
-LOADS = [["x",0],["x",1],["x",2],["w",0],["x",3],["w",1],["w",2],["g",0],["w",3],["g",1],["g",2],["g",3]]
-W_ON_VECTOR = ()
-W_FIRST = (0,)
+W_PIECES = [1,1,2,2,2]
+W_FIRSTS = [sum(W_PIECES[:i]) for i in range(len(W_PIECES))]
+LOADS = [["x",0],["x",1],["x",2],["w",0],["x",3],["w",1],["w",2],["w",3],["g",0],["w",4],["g",1],["g",2],["g",3]]
 
 
 def tile_routed_moe_kernel(tc, xT, w, gate, offs, out):
@@ -45,8 +45,8 @@ def tile_routed_moe_kernel(tc, xT, w, gate, offs, out):
                 x_planes[i] = held.tile([P, T], F32, name="x_plane%d" % i)
                 nc.sync.dma_start(x_planes[i][:], x_rows[:, i, :])
             elif kind == "w":
-                w_raw[i] = held.tile([P, E_CHUNK, PACK, N], F32, name="w_raw%d" % i)
-                nc.sync.dma_start(w_raw[i][:], w_rows[:, i * E_CHUNK : (i + 1) * E_CHUNK, :, :])
+                w_raw[i] = held.tile([P, W_PIECES[i], PACK, N], F32, name="w_raw%d" % i)
+                nc.sync.dma_start(w_raw[i][:], w_rows[:, W_FIRSTS[i] : W_FIRSTS[i] + W_PIECES[i], :, :])
             else:
                 gate_sb[i] = held.tile([P, CHUNK], F32, name="gate%d" % i)
                 nc.sync.dma_start(gate_sb[i][:], gate[:, i * CHUNK : (i + 1) * CHUNK])
@@ -57,40 +57,26 @@ def tile_routed_moe_kernel(tc, xT, w, gate, offs, out):
         def offs_of(first_slot, n_slots):
             return offsets[:, first_slot // 16 : (first_slot + n_slots) // 16]
 
-        w_grouped = {}
+        w_grouped = [held.tile([P, CHUNK, PACK], BF16, name="w_grouped%d" % c, align_bytes=64) for c in range(N_CHUNKS)]
 
-        def interleave_w(c):
-            w_grouped[c] = held.tile([P, CHUNK, PACK], BF16, name="w_grouped%d" % c, align_bytes=64)
-            w_out = w_grouped[c][:].rearrange("p (e b i) j -> p e b j i", e=E_CHUNK, i=4)
-            w_in = w_raw[c][:].rearrange("p e j (b i) -> p e b j i", i=4)
-            if c in W_ON_VECTOR:
-                nc.vector.tensor_copy(out=w_out, in_=w_in)
-            else:
-                nc.scalar.copy(out=w_out, in_=w_in)
-
-        w_codes = {}
-        w_scales = {}
-
-        def quantize_w(c):
-            w_codes[c] = held.tile([P, CHUNK], U32, name="w_codes%d" % c, align_bytes=64)
-            w_scales[c] = held.tile([P, CHUNK], U8, name="w_scales%d" % c, align_bytes=64)
-            nc.vector.quantize_mx(
-                out=w_codes[c][:].bitcast(FP8X4),
-                scales=w_scales[c][:],
-                in_=w_grouped[c][:].rearrange("p n j -> p (n j)"),
+        def interleave_w(i):
+            c = W_FIRSTS[i] // E_CHUNK
+            first = (W_FIRSTS[i] % E_CHUNK) * N
+            nc.scalar.copy(
+                out=w_grouped[c][:, first : first + W_PIECES[i] * N, :].rearrange(
+                    "p (e b i) j -> p e b j i", e=W_PIECES[i], i=4
+                ),
+                in_=w_raw[i][:].rearrange("p e j (b i) -> p e b j i", i=4),
             )
 
-        for c in W_FIRST:
-            interleave_w(c)
+        interleave_w(0)
 
         early = [held.tile([P, 2, EARLY], F32, name="early%d" % h) for h in range(SLOTS // EARLY)]
         for t in range(2):
             for h in range(SLOTS // EARLY):
                 nc.vector.tensor_copy(early[h][:, t, :], x_planes[t][:].indirect(offs_of(h * EARLY, EARLY)))
 
-        x_grouped = [
-            held.tile([P, CHUNK, PACK], BF16, name="x_grouped%d" % c, align_bytes=64) for c in range(N_CHUNKS)
-        ]
+        x_grouped = [held.tile([P, CHUNK, PACK], BF16, name="x_grouped%d" % c, align_bytes=64) for c in range(N_CHUNKS)]
         for c in range(N_CHUNKS):
             first = c * CHUNK % EARLY
             nc.scalar.copy(
@@ -99,16 +85,15 @@ def tile_routed_moe_kernel(tc, xT, w, gate, offs, out):
             )
 
         late = [held.tile([P, 2, CHUNK], F32, name="late%d" % c) for c in range(N_CHUNKS)]
-        for c in range(N_CHUNKS):
-            nc.vector.tensor_copy(late[c][:, 0, :], x_planes[2][:].indirect(offs_of(c * CHUNK, CHUNK)))
-        for c in W_FIRST:
-            quantize_w(c)
+        for t in range(2):
+            for c in range(N_CHUNKS):
+                nc.vector.tensor_copy(late[c][:, t, :], x_planes[2 + t][:].indirect(offs_of(c * CHUNK, CHUNK)))
 
         for c in range(N_CHUNKS):
-            nc.vector.tensor_copy(late[c][:, 1, :], x_planes[3][:].indirect(offs_of(c * CHUNK, CHUNK)))
             nc.scalar.copy(out=x_grouped[c][:, :, 2:4], in_=late[c][:].rearrange("p t n -> p n t"))
-            if c not in W_FIRST:
-                interleave_w(c)
+            for i in range(1, len(W_PIECES)):
+                if W_FIRSTS[i] // E_CHUNK == c:
+                    interleave_w(i)
 
             x_codes = held.tile([P, CHUNK], U32, name="x_codes%d" % c, align_bytes=64)
             x_scales = held.tile([P, CHUNK], U8, name="x_scales%d" % c, align_bytes=64)
@@ -117,16 +102,21 @@ def tile_routed_moe_kernel(tc, xT, w, gate, offs, out):
                 scales=x_scales[:],
                 in_=x_grouped[c][:].rearrange("p n t -> p (n t)"),
             )
-            if c not in W_FIRST:
-                quantize_w(c)
+            w_codes = held.tile([P, CHUNK], U32, name="w_codes%d" % c, align_bytes=64)
+            w_scales = held.tile([P, CHUNK], U8, name="w_scales%d" % c, align_bytes=64)
+            nc.vector.quantize_mx(
+                out=w_codes[:].bitcast(FP8X4),
+                scales=w_scales[:],
+                in_=w_grouped[c][:].rearrange("p n j -> p (n j)"),
+            )
 
             sums = psum.tile([P, CHUNK], F32, name="sums%d" % c)
             for i in range(E_CHUNK):
                 cols = slice(i * C, (i + 1) * C)
                 nc.tensor.matmul_mx(
                     out=sums[:, cols],
-                    lhsT=w_codes[c][:, cols].bitcast(FP8X4),
-                    lhsT_scale=w_scales[c][:, cols],
+                    lhsT=w_codes[:, cols].bitcast(FP8X4),
+                    lhsT_scale=w_scales[:, cols],
                     rhs=x_codes[:, cols].bitcast(FP8X4),
                     rhs_scale=x_scales[:, cols],
                     start=True,

@@ -13,6 +13,7 @@ U16 = mybir.dt.uint16
 U8 = mybir.dt.uint8
 FP8X4 = mybir.dt.float8_e4m3fn_x4
 MULT = mybir.AluOpType.mult
+COPY = mybir.ActivationFunctionType.Copy
 
 P = 128
 PACK = 4
@@ -21,9 +22,9 @@ CHUNK = 256
 N_CHUNKS = SLOTS // CHUNK
 E_CHUNK = CHUNK // C
 
-W_PIECES = [1,1,2,2,2]
+W_PIECES = [1, 1, 2, 2, 2]
 W_FIRSTS = [sum(W_PIECES[:i]) for i in range(len(W_PIECES))]
-LOADS = [["x",0],["x",1],["x",2],["w",0],["x",3],["w",1],["w",2],["w",3],["g",0],["w",4],["g",1],["g",2],["g",3]]
+LOADS = [["x", 0], ["o", 0], ["x", 1], ["x", 2], ["w", 0], ["x", 3], ["w", 1], ["w", 2], ["w", 3], ["g", 0], ["w", 4], ["g", 1], ["g", 2], ["g", 3]]
 
 
 def tile_routed_moe_kernel(tc, xT, w, gate, offs, out):
@@ -33,7 +34,6 @@ def tile_routed_moe_kernel(tc, xT, w, gate, offs, out):
         psum = ctx.enter_context(tc.psum_pool(name="psum", bufs=1))
 
         offsets = held.tile([P, SLOTS // 16], U16, name="offsets")
-        nc.sync.dma_start(offsets[:], offs)
 
         x_rows = xT.rearrange("(p t) n -> p t n", t=PACK)
         w_rows = w.rearrange("e (p j) n -> p e j n", j=PACK)
@@ -41,7 +41,9 @@ def tile_routed_moe_kernel(tc, xT, w, gate, offs, out):
         w_raw = {}
         gate_sb = {}
         for kind, i in LOADS:
-            if kind == "x":
+            if kind == "o":
+                nc.sync.dma_start(offsets[:], offs)
+            elif kind == "x":
                 x_planes[i] = held.tile([P, T], F32, name="x_plane%d" % i)
                 nc.sync.dma_start(x_planes[i][:], x_rows[:, i, :])
             elif kind == "w":
@@ -84,17 +86,12 @@ def tile_routed_moe_kernel(tc, xT, w, gate, offs, out):
                 in_=early[c * CHUNK // EARLY][:, :, first : first + CHUNK].rearrange("p t n -> p n t"),
             )
 
-        late = [held.tile([P, 2, CHUNK], F32, name="late%d" % c) for c in range(N_CHUNKS)]
-        for t in range(2):
-            for c in range(N_CHUNKS):
-                nc.vector.tensor_copy(late[c][:, t, :], x_planes[2 + t][:].indirect(offs_of(c * CHUNK, CHUNK)))
-
+        late = held.tile([P, 2, SLOTS], F32, name="late")
+        nc.vector.tensor_copy(late[:, 0, :], x_planes[2][:].indirect(offsets[:]))
         for c in range(N_CHUNKS):
-            nc.scalar.copy(out=x_grouped[c][:, :, 2:4], in_=late[c][:].rearrange("p t n -> p n t"))
-            for i in range(1, len(W_PIECES)):
-                if W_FIRSTS[i] // E_CHUNK == c:
-                    interleave_w(i)
+            nc.vector.tensor_copy(late[:, 1, c * CHUNK : (c + 1) * CHUNK], x_planes[3][:].indirect(offs_of(c * CHUNK, CHUNK)))
 
+        def finish_chunk(c):
             x_codes = held.tile([P, CHUNK], U32, name="x_codes%d" % c, align_bytes=64)
             x_scales = held.tile([P, CHUNK], U8, name="x_scales%d" % c, align_bytes=64)
             nc.vector.quantize_mx(
@@ -125,5 +122,12 @@ def tile_routed_moe_kernel(tc, xT, w, gate, offs, out):
             sums_sb = held.tile([P, CHUNK], F32, name="sums_sb%d" % c)
             nc.scalar.copy(out=sums_sb[:], in_=sums[:])
             nc.vector.tensor_tensor(window[:].indirect(offs_of(c * CHUNK, CHUNK)), sums_sb[:], gate_sb[c][:], MULT)
+
+        for c in range(N_CHUNKS):
+            nc.scalar.copy(out=x_grouped[c][:, :, 2:4], in_=late[:, :, c * CHUNK : (c + 1) * CHUNK].rearrange("p t n -> p n t"))
+            for i in range(1, len(W_PIECES)):
+                if W_FIRSTS[i] // E_CHUNK == c:
+                    interleave_w(i)
+            finish_chunk(c)
 
         nc.sync.dma_start(out, window[:])

@@ -73,17 +73,16 @@ def tile_routed_moe_kernel(tc, xT, w, gate, offs, out):
 
         interleave_w(0)
 
-        early = [held.tile([P, 2, EARLY], F32, name="early%d" % h) for h in range(SLOTS // EARLY)]
-        for t in range(2):
-            for h in range(SLOTS // EARLY):
-                nc.vector.tensor_copy(early[h][:, t, :], x_planes[t][:].indirect(offs_of(h * EARLY, EARLY)))
+        early = held.tile([P, 2, SLOTS], F32, name="early")
+        nc.vector.tensor_copy(early[:, 0, :], x_planes[0][:].indirect(offsets[:]))
+        for h in range(SLOTS // EARLY):
+            nc.vector.tensor_copy(early[:, 1, h * EARLY : (h + 1) * EARLY], x_planes[1][:].indirect(offs_of(h * EARLY, EARLY)))
 
         x_grouped = [held.tile([P, CHUNK, PACK], BF16, name="x_grouped%d" % c, align_bytes=64) for c in range(N_CHUNKS)]
         for c in range(N_CHUNKS):
-            first = c * CHUNK % EARLY
             nc.scalar.copy(
                 out=x_grouped[c][:, :, 0:2],
-                in_=early[c * CHUNK // EARLY][:, :, first : first + CHUNK].rearrange("p t n -> p n t"),
+                in_=early[:, :, c * CHUNK : (c + 1) * CHUNK].rearrange("p t n -> p n t"),
             )
 
         late = held.tile([P, 2, SLOTS], F32, name="late")

@@ -45,7 +45,7 @@ def tile_routed_moe_kernel(tc, xT, w, gate, offs, out):
                 nc.sync.dma_start(offsets[:], offs)
             elif kind == "x":
                 x_planes[i] = held.tile([P, T], F32, name="x_plane%d" % i)
-                nc.sync.dma_start(x_planes[i][:], x_rows[:, i, :])
+                (nc.scalar if i == 0 else nc.sync).dma_start(x_planes[i][:], x_rows[:, i, :])
             elif kind == "w":
                 w_raw[i] = held.tile([P, W_PIECES[i], PACK, N], F32, name="w_raw%d" % i)
                 nc.sync.dma_start(w_raw[i][:], w_rows[:, W_FIRSTS[i] : W_FIRSTS[i] + W_PIECES[i], :, :])

@@ -22,6 +22,7 @@ CHUNK = 256
 N_CHUNKS = SLOTS // CHUNK
 E_CHUNK = CHUNK // C
 
+LAST_GATHERS = [(0, 256), (256, 256), (512, 512)]
 W_PIECES = [1, 1, 2, 2, 2]
 W_FIRSTS = [sum(W_PIECES[:i]) for i in range(len(W_PIECES))]
 LOADS = [["x", 0], ["o", 0], ["x", 1], ["x", 2], ["w", 0], ["x", 3], ["w", 1], ["w", 2], ["w", 3], ["g", 0], ["w", 4], ["g", 1], ["g", 2], ["g", 3]]
@@ -87,8 +88,8 @@ def tile_routed_moe_kernel(tc, xT, w, gate, offs, out):
 
         late = held.tile([P, 2, SLOTS], F32, name="late")
         nc.vector.tensor_copy(late[:, 0, :], x_planes[2][:].indirect(offsets[:]))
-        for c in range(N_CHUNKS):
-            nc.vector.tensor_copy(late[:, 1, c * CHUNK : (c + 1) * CHUNK], x_planes[3][:].indirect(offs_of(c * CHUNK, CHUNK)))
+        for first, n in LAST_GATHERS:
+            nc.vector.tensor_copy(late[:, 1, first : first + n], x_planes[3][:].indirect(offs_of(first, n)))
 
         def finish_chunk(c):
             x_codes = held.tile([P, CHUNK], U32, name="x_codes%d" % c, align_bytes=64)

from contextlib import ExitStack

import concourse.mybir as mybir

K, T, E, C, N = 512, 2048, 8, 128, 128
SLOTS = E * C
FLOPS = 2 * K * N * SLOTS

F32 = mybir.dt.float32
BF16 = mybir.dt.bfloat16
U32 = mybir.dt.uint32
U16 = mybir.dt.uint16
U8 = mybir.dt.uint8
FP8X4 = mybir.dt.float8_e4m3fn_x4
MULT = mybir.AluOpType.mult
COPY = mybir.ActivationFunctionType.Copy

P = 128
PACK = 4
EARLY = 512
CHUNK = 256
N_CHUNKS = SLOTS // CHUNK
E_CHUNK = CHUNK // C

LAST_GATHERS = [(0, 256), (256, 256), (512, 512)]
W_PIECES = [1, 1, 2, 2, 2]
W_FIRSTS = [sum(W_PIECES[:i]) for i in range(len(W_PIECES))]
LOADS = [["x", 0], ["o", 0], ["x", 1], ["x", 2], ["w", 0], ["x", 3], ["w", 1], ["w", 2], ["w", 3], ["g", 0], ["w", 4], ["g", 1], ["g", 2], ["g", 3]]


def tile_routed_moe_kernel(tc, xT, w, gate, offs, out):
    nc = tc.nc
    with ExitStack() as ctx:
        held = ctx.enter_context(tc.tile_pool(name="held", bufs=1))
        psum = ctx.enter_context(tc.psum_pool(name="psum", bufs=1))

        offsets = held.tile([P, SLOTS // 16], U16, name="offsets")

        x_rows = xT.rearrange("(p t) n -> p t n", t=PACK)
        w_rows = w.rearrange("e (p j) n -> p e j n", j=PACK)
        x_planes = {}
        w_raw = {}
        gate_sb = {}
        for kind, i in LOADS:
            if kind == "o":
                nc.sync.dma_start(offsets[:], offs)
            elif kind == "x":
                x_planes[i] = held.tile([P, T], F32, name="x_plane%d" % i)
                (nc.scalar if i == 0 else nc.sync).dma_start(x_planes[i][:], x_rows[:, i, :])
            elif kind == "w":
                w_raw[i] = held.tile([P, W_PIECES[i], PACK, N], F32, name="w_raw%d" % i)
                nc.sync.dma_start(w_raw[i][:], w_rows[:, W_FIRSTS[i] : W_FIRSTS[i] + W_PIECES[i], :, :])
            else:
                gate_sb[i] = held.tile([P, CHUNK], F32, name="gate%d" % i)
                nc.sync.dma_start(gate_sb[i][:], gate[:, i * CHUNK : (i + 1) * CHUNK])

        window = held.tile([P, T], F32, name="window")
        nc.vector.memset(window[:], 0.0)

        def offs_of(first_slot, n_slots):
            return offsets[:, first_slot // 16 : (first_slot + n_slots) // 16]

        w_grouped = [held.tile([P, CHUNK, PACK], BF16, name="w_grouped%d" % c, align_bytes=64) for c in range(N_CHUNKS)]

        def interleave_w(i):
            c = W_FIRSTS[i] // E_CHUNK
            first = (W_FIRSTS[i] % E_CHUNK) * N
            nc.scalar.copy(
                out=w_grouped[c][:, first : first + W_PIECES[i] * N, :].rearrange(
                    "p (e b i) j -> p e b j i", e=W_PIECES[i], i=4
                ),
                in_=w_raw[i][:].rearrange("p e j (b i) -> p e b j i", i=4),
            )

        interleave_w(0)

        early = held.tile([P, 2, SLOTS], F32, name="early")
        nc.vector.tensor_copy(early[:, 0, :], x_planes[0][:].indirect(offsets[:]))
        for h in range(SLOTS // EARLY):
            nc.vector.tensor_copy(early[:, 1, h * EARLY : (h + 1) * EARLY], x_planes[1][:].indirect(offs_of(h * EARLY, EARLY)))

        x_grouped = [held.tile([P, CHUNK, PACK], BF16, name="x_grouped%d" % c, align_bytes=64) for c in range(N_CHUNKS)]
        for c in range(N_CHUNKS):
            nc.scalar.copy(
                out=x_grouped[c][:, :, 0:2],
                in_=early[:, :, c * CHUNK : (c + 1) * CHUNK].rearrange("p t n -> p n t"),
            )

        late = held.tile([P, 2, SLOTS], F32, name="late")
        nc.vector.tensor_copy(late[:, 0, :], x_planes[2][:].indirect(offsets[:]))
        for first, n in LAST_GATHERS:
            nc.vector.tensor_copy(late[:, 1, first : first + n], x_planes[3][:].indirect(offs_of(first, n)))

        def finish_chunk(c):
            x_codes = held.tile([P, CHUNK], U32, name="x_codes%d" % c, align_bytes=64)
            x_scales = held.tile([P, CHUNK], U8, name="x_scales%d" % c, align_bytes=64)
            nc.vector.quantize_mx(
                out=x_codes[:].bitcast(FP8X4),
                scales=x_scales[:],
                in_=x_grouped[c][:].rearrange("p n t -> p (n t)"),
            )
            w_codes = held.tile([P, CHUNK], U32, name="w_codes%d" % c, align_bytes=64)
            w_scales = held.tile([P, CHUNK], U8, name="w_scales%d" % c, align_bytes=64)
            nc.vector.quantize_mx(
                out=w_codes[:].bitcast(FP8X4),
                scales=w_scales[:],
                in_=w_grouped[c][:].rearrange("p n j -> p (n j)"),
            )

            sums = psum.tile([P, CHUNK], F32, name="sums%d" % c)
            for i in range(E_CHUNK):
                cols = slice(i * C, (i + 1) * C)
                nc.tensor.matmul_mx(
                    out=sums[:, cols],
                    lhsT=w_codes[:, cols].bitcast(FP8X4),
                    lhsT_scale=w_scales[:, cols],
                    rhs=x_codes[:, cols].bitcast(FP8X4),
                    rhs_scale=x_scales[:, cols],
                    start=True,
                    stop=True,
                )
            sums_sb = held.tile([P, CHUNK], F32, name="sums_sb%d" % c)
            nc.scalar.copy(out=sums_sb[:], in_=sums[:])
            nc.vector.tensor_tensor(window[:].indirect(offs_of(c * CHUNK, CHUNK)), sums_sb[:], gate_sb[c][:], MULT)

        for c in range(N_CHUNKS):
            nc.scalar.copy(out=x_grouped[c][:, :, 2:4], in_=late[:, :, c * CHUNK : (c + 1) * CHUNK].rearrange("p t n -> p n t"))
            for i in range(1, len(W_PIECES)):
                if W_FIRSTS[i] // E_CHUNK == c:
                    interleave_w(i)
            finish_chunk(c)

        nc.sync.dma_start(out, window[:])
